import numpy as np
import ml_dtypes


def mxq(x, axis, fmt="e4m3"):
    dtype, down = {"e4m3": (ml_dtypes.float8_e4m3fn, 7), "e5m2": (ml_dtypes.float8_e5m2, 14)}[fmt]
    v = np.moveaxis(np.asarray(x, np.float32).astype(ml_dtypes.bfloat16).astype(np.float64), axis, -1)
    blocks = v.reshape(v.shape[:-1] + (-1, 32))
    amax = np.abs(blocks).max(-1, keepdims=True)
    byte = np.maximum(np.where(amax > 0, np.frexp(amax)[1] - 1 + 127, 0) - down, 1)
    scale = np.exp2(byte - 127.0)
    codes = (blocks / scale).astype(np.float32).astype(dtype).astype(np.float64)
    return np.moveaxis((codes * scale).reshape(v.shape), -1, axis)


WIDE = False


def mx_kscale(k):
    if not WIDE:
        return np.ones(k)
    levels = np.array([10, -10, 5, -5, 0])
    if k % 512:
        return np.exp2(np.random.permutation(np.resize(levels, k // 32))).repeat(32)
    a = np.empty((k // 512, 16))
    for p in range(k // 512):
        a[p, :8] = np.random.permutation(np.resize(levels, 8))
        for g in range(8):
            far = levels[np.abs(levels - a[p, g]) >= 10]
            a[p, g + 8] = far[np.random.randint(len(far))]
    return np.exp2(a.ravel()).repeat(32)


BF16 = ml_dtypes.bfloat16


def bf(x):
    return np.asarray(x, np.float32).astype(BF16)


def f64(x):
    return np.asarray(x).astype(np.float64)


E2M1 = np.array([0.0, 0.5, 1.0, 1.5, 2.0, 3.0, 4.0, 6.0, -0.0, -0.5, -1.0, -1.5, -2.0, -3.0, -4.0, -6.0])


def pack_weight(w, fmt):
    k, n = w.shape
    w = f64(bf(w)).reshape(k // 32, 32, n)
    amax = np.abs(w).max(1)
    if fmt == "e4m3":
        byte = np.frexp(amax)[1] - 1 + 127 - 7
    else:
        mant, ex = np.frexp(amax / 6.0)
        byte = np.where(mant > 0.5, ex, ex - 1) + 127
    byte = np.clip(np.where(amax > 0, byte, 1), 1, 254)
    scaled = (w * np.exp2(127.0 - byte)[:, None, :]).reshape(k, n).astype(np.float32)
    by_word = np.ascontiguousarray(scaled.reshape(k // 512, 128, 4, n).transpose(0, 1, 3, 2))
    if fmt == "e4m3":
        words = by_word.astype(ml_dtypes.float8_e4m3fn).view(np.uint8)
    else:
        c = by_word.astype(ml_dtypes.float4_e2m1fn).view(np.uint8) & 0xF
        words = c[..., 0::2] | (c[..., 1::2] << 4)
    return np.ascontiguousarray(words), np.ascontiguousarray(byte.astype(np.uint8).reshape(k // 512, 16, n))


def unpack_weight(words, scales, fmt):
    g, p, n, _ = words.shape
    if fmt == "e4m3":
        vals = np.ascontiguousarray(words).view(ml_dtypes.float8_e4m3fn).astype(np.float64)
    else:
        nib = np.empty((g, p, n, 4), np.uint8)
        nib[..., 0::2] = words & 0xF
        nib[..., 1::2] = words >> 4
        vals = E2M1[nib]
    vals = vals * np.repeat(np.exp2(scales.astype(np.float64) - 127.0), 8, axis=1)[..., None]
    return vals.transpose(0, 1, 3, 2).reshape(g * 512, n)
def pack4(w):
    words, scales = pack_weight(w, "e2m1")
    return words.reshape(words.shape[0], 128, -1), scales


def unpack4(words, scales):
    return unpack_weight(words.reshape(words.shape[0], 128, -1, 2), scales, "e2m1")


G, P, T = 4, 1024, 512


def setup_inputs():
    s = mx_kscale(G * P)
    ff = np.random.standard_normal((G * P, P)) / np.sqrt(P) * s[:, None]
    ff_words, ff_scales = pack4(ff)
    sr = s.reshape(G, P)
    return {"emission": bf(np.abs(np.random.standard_normal((G, T, P))) / sr[:, None, :]),
            "ff_words": ff_words,
            "ff_scales": ff_scales,
            "ambient": bf(0.3 * np.abs(np.random.standard_normal((G, P)))),
            "rho": bf(np.random.uniform(0.3, 0.9, (G, P)) / sr)}


def reference(emission, ff_words, ff_scales, ambient, rho):
    ff = unpack4(ff_words, ff_scales).reshape(G, P, P)
    e = mxq(f64(emission), 2, "e4m3")
    direct = e @ ff
    h = np.maximum(direct + f64(ambient)[:, None, :], 0.0)
    b = h * f64(rho)[:, None, :]
    second = mxq(b, 2, "e4m3") @ ff
    return h + second

@@ -1,0 +1,289 @@
+from contextlib import ExitStack
+
+import concourse.mybir as mybir
+from concourse.masks import make_identity
+
+ROOMS, STATES, PATCHES = 4, 512, 1024
+FLOPS = 2 * 2 * ROOMS * STATES * PATCHES * PATCHES
+
+F32 = mybir.dt.float32
+BF16 = mybir.dt.bfloat16
+I32 = mybir.dt.int32
+U32 = mybir.dt.uint32
+U8 = mybir.dt.uint8
+FP8X4 = mybir.dt.float8_e4m3fn_x4
+FP4X4 = mybir.dt.float4_e2m1fn_x4
+ALU = mybir.AluOpType
+ACT = mybir.ActivationFunctionType
+
+P = 128
+HALF = 512
+PASSES = PATCHES // HALF
+TILES_PER_ROOM = STATES // P
+TILES = ROOMS * TILES_PER_ROOM
+LAG_T = 2
+LAG_M = 3
+SHARE = 4
+SHARE_FIRST = 4
+N_FIRST = 1
+SHARE_LAST = 2
+SORT_E = 0
+
+
+def tile_two_bounce_signed_transfer_s14_kernel(tc, emission, ff_words, ff_scales, ambient, rho, out):
+    nc = tc.nc
+    with ExitStack() as ctx:
+        sbuf = ctx.enter_context(tc.tile_pool(name="sbuf", bufs=1))
+        psum = ctx.enter_context(tc.psum_pool(name="psum", bufs=1))
+        ctx.enter_context(tc.manual_schedule())
+
+        def slot(pool, kind, index, slots, shape, dtype):
+            name = "%s%d" % (kind, index % slots)
+            return pool.tile(shape, dtype, name=name, tag=name, align_bytes=64)
+
+        def bank(kind, index, slots):
+            name = "%s%d" % (kind, index % slots)
+            return psum.tile([P, HALF], F32, name=name, tag=name)
+
+        identity = sbuf.tile([P, P], F32, name="identity", align_bytes=64)
+        make_identity(nc, identity[:])
+
+        first_scales = sbuf.tile([P, PASSES * PATCHES], U8, name="first_scales", align_bytes=64)
+        later_scales = sbuf.tile([P, (ROOMS - 1) * PASSES * PATCHES], U8, name="later_scales", align_bytes=64)
+        nc.vector.memset(first_scales[:].bitcast(I32), 0)
+        nc.vector.memset(later_scales[:].bitcast(I32), 0)
+
+        emitted, weights, ambient_rows, rho_rows, rho_sorted = {}, {}, {}, {}, {}
+        received, clamped, sent, turned, codes, scales = {}, {}, {}, {}, {}, {}
+        direct, second, ordered, grouped = {}, {}, {}, {}
+
+        def load_emission(i):
+            room, row = divmod(i, TILES_PER_ROOM)
+            emitted[i] = slot(sbuf, "emitted", i, TILES, [P, PATCHES], BF16)
+            nc.sync.dma_start(out=emitted[i][:], in_=emission[room, row * P:(row + 1) * P, :])
+
+        def load_weights(group):
+            weights[group] = slot(sbuf, "weights", group, ROOMS * PASSES, [P, 2 * PATCHES], U8)
+            nc.sync.dma_start(out=weights[group][:].bitcast(I32), in_=ff_words[group].bitcast(I32))
+
+        def load_scales(plane, first_group, groups):
+            for quadrant in range(4):
+                nc.sync.dma_start(
+                    out=plane[32 * quadrant:32 * quadrant + 4, :].bitcast(I32).rearrange("q (g n) -> q g n", g=groups),
+                    in_=ff_scales[first_group:first_group + groups, 4 * quadrant:4 * quadrant + 4, :]
+                    .bitcast(I32).rearrange("g q n -> q g n"),
+                )
+
+        def load_row(store, kind, source, room):
+            store[room] = slot(sbuf, kind, room, ROOMS, [P, PATCHES], BF16)
+            nc.sync.dma_start(out=store[room][:], in_=source[room].partition_broadcast(P))
+
+        def load_room(room):
+            first = room * TILES_PER_ROOM
+            load_emission(first)
+            for g in range(PASSES):
+                load_weights(room * PASSES + g)
+            load_row(ambient_rows, "ambient", ambient, room)
+            load_emission(first + 1)
+            load_row(rho_rows, "rho", rho, room)
+            for i in range(first + 2, first + TILES_PER_ROOM):
+                load_emission(i)
+
+        def weight_scales(room, g, half):
+            if room == 0:
+                plane, start = first_scales, g * PATCHES
+            else:
+                plane, start = later_scales, ((room - 1) * PASSES + g) * PATCHES
+            return plane[:, start + half * HALF:start + (half + 1) * HALF]
+
+        def sort_rho(room, g):
+            rho_sorted[room, g] = slot(sbuf, "rho_sorted", PASSES * room + g, 2 * PASSES, [P, HALF], F32)
+            nc.scalar.copy(
+                out=rho_sorted[room, g][:].rearrange("p (u m e) -> p u m e", u=2, e=2),
+                in_=rho_rows[room][:, g * HALF:(g + 1) * HALF].rearrange("p (m u e) -> p u m e", u=2, e=2),
+            )
+
+        def sort_emission(i):
+            ordered[i] = slot(sbuf, "ordered", i, 2, [P, HALF], F32)
+            nc.scalar.copy(
+                out=ordered[i][:].rearrange("p (g u m) -> p g u m", g=PASSES, u=2),
+                in_=emitted[i][:].bitcast(F32).rearrange("p (g m u) -> p g u m", g=PASSES, u=2),
+            )
+
+        def turn_emission(i):
+            turned["e", i] = bank("turned", len(turned), 2)
+            words = emitted[i][:].bitcast(F32)
+            for g in range(PASSES):
+                for u in range(2):
+                    nc.tensor.transpose(
+                        turned["e", i][:, (2 * g + u) * P:(2 * g + u + 1) * P],
+                        ordered[i][:, (2 * g + u) * P:(2 * g + u + 1) * P] if i in ordered
+                        else words[:, 2 * P * g + u:2 * P * (g + 1):2],
+                        identity[:],
+                    )
+
+        def turn_sent(i):
+            turned["b", i] = bank("turned", len(turned), 2)
+            for g in range(PASSES):
+                words = sent[i, g][:].bitcast(F32)
+                for u in range(2):
+                    nc.tensor.transpose(
+                        turned["b", i][:, (2 * g + u) * P:(2 * g + u + 1) * P],
+                        words[:, u * P:(u + 1) * P],
+                        identity[:],
+                    )
+
+        def group(step, operands):
+            grouped[step] = slot(sbuf, "grouped", step, 2, [P, 2 * PATCHES], BF16)
+            for n, key in enumerate(operands):
+                nc.scalar.copy(
+                    out=grouped[step][:, n * PATCHES:(n + 1) * PATCHES].bitcast(F32).rearrange("p (g s u) -> p g s u", g=PASSES, u=2),
+                    in_=turned[key][:].rearrange("p (g u s) -> p g s u", g=PASSES, u=2),
+                )
+
+        def quantize(step, operands):
+            width = len(operands) * PASSES * P
+            step_codes = slot(sbuf, "codes", step, 3, [P, 2 * PASSES * P], U32)
+            step_scales = slot(sbuf, "scales", step, 3, [P, 2 * PASSES * P], U8)
+            for n, key in enumerate(operands):
+                codes[key] = step_codes[:, n * PASSES * P:(n + 1) * PASSES * P]
+                scales[key] = step_scales[:, n * PASSES * P:(n + 1) * PASSES * P]
+            nc.vector.quantize_mx(
+                out=step_codes[:, :width].bitcast(FP8X4), scales=step_scales[:, :width], in_=grouped[step][:, :4 * width]
+            )
+
+        def bounce(kind, i, sums):
+            room = i // TILES_PER_ROOM
+            for half in range(PASSES):
+                sums[i, half] = bank("sums_" + kind, PASSES * i + half, 3)
+                for g in range(PASSES):
+                    nc.tensor.matmul_mx(
+                        out=sums[i, half][:],
+                        lhsT=codes[kind, i][:, g * P:(g + 1) * P].bitcast(FP8X4),
+                        lhsT_scale=scales[kind, i][:, g * P:(g + 1) * P],
+                        rhs=weights[room * PASSES + g][:, 2 * half * HALF:2 * (half + 1) * HALF].bitcast(FP4X4),
+                        rhs_scale=weight_scales(room, g, half),
+                        start=(g == 0),
+                        stop=(g == PASSES - 1),
+                    )
+
+        def add_ambient(i, half):
+            room = i // TILES_PER_ROOM
+            received[i, half] = slot(sbuf, "received", PASSES * i + half, PASSES * (LAG_M + 2), [P, HALF], F32)
+            nc.vector.tensor_tensor(
+                out=received[i, half][:],
+                in0=ambient_rows[room][:, half * HALF:(half + 1) * HALF],
+                in1=direct[i, half][:],
+                op=ALU.add,
+            )
+            sent[i, half] = slot(sbuf, "sent", PASSES * i + half, 6, [P, HALF], BF16)
+
+        def gpsimd_runs(i, half):
+            quarters = SHARE_FIRST if i < N_FIRST else SHARE_LAST if i == TILES - 1 else SHARE
+            return max(0, min(2, quarters - 2 * half))
+
+        def send_on_vector(i, half):
+            room = i // TILES_PER_ROOM
+            pairs = received[i, half][:].rearrange("p (m u e) -> p u m e", u=2, e=2)
+            for u in range(gpsimd_runs(i, half), 2):
+                cols = slice(u * 2 * P, (u + 1) * 2 * P)
+                nc.vector.scalar_tensor_tensor(
+                    out=sent[i, half][:, cols].rearrange("p (m e) -> p m e", e=2),
+                    in0=pairs[:, u],
+                    scalar=0.0,
+                    in1=rho_sorted[room, half][:, cols].rearrange("p (m e) -> p m e", e=2),
+                    op0=ALU.max,
+                    op1=ALU.mult,
+                )
+
+        def clamp(i, half):
+            runs = gpsimd_runs(i, half)
+            if runs > 0:
+                pairs = received[i, half][:].rearrange("p (m u e) -> p u m e", u=2, e=2)
+                clamped[i, half] = slot(sbuf, "clamped", PASSES * i + half, 4, [P, HALF], F32)
+                nc.scalar.activation(
+                    out=clamped[i, half][:, :runs * 2 * P].rearrange("p (u m e) -> p u m e", u=runs, e=2),
+                    in_=pairs[:, :runs],
+                    func=ACT.Relu,
+                )
+
+        def send_on_gpsimd(i, half):
+            room = i // TILES_PER_ROOM
+            width = gpsimd_runs(i, half) * 2 * P
+            if width > 0:
+                nc.gpsimd.tensor_tensor(
+                    out=sent[i, half][:, :width],
+                    in0=clamped[i, half][:, :width],
+                    in1=rho_sorted[room, half][:, :width],
+                    op=ALU.mult,
+                )
+
+        def finish(i):
+            room, row = divmod(i, TILES_PER_ROOM)
+            for half in range(PASSES):
+                result = slot(sbuf, "result", PASSES * i + half, 8, [P, HALF], F32)
+                nc.vector.scalar_tensor_tensor(
+                    out=result[:],
+                    in0=received[i, half][:],
+                    scalar=0.0,
+                    in1=second[i, half][:],
+                    op0=ALU.max,
+                    op1=ALU.add,
+                )
+                nc.sync.dma_start(
+                    out=out[room, row * P:(row + 1) * P, half * HALF:(half + 1) * HALF], in_=result[:]
+                )
+
+        load_emission(0)
+        load_emission(1)
+        load_scales(first_scales, 0, PASSES)
+        for g in range(PASSES):
+            load_weights(g)
+        load_row(ambient_rows, "ambient", ambient, 0)
+        load_emission(2)
+        load_row(rho_rows, "rho", rho, 0)
+        load_emission(3)
+        load_scales(later_scales, PASSES, (ROOMS - 1) * PASSES)
+        for room in range(1, ROOMS):
+            load_room(room)
+
+        turn_emission(0)
+        group(-1, [("e", 0)])
+        quantize(-1, [("e", 0)])
+        for step in range(TILES + LAG_M):
+            ahead, before, late, last = step + 1, step - 1, step - LAG_T, step - LAG_M
+            if 0 <= before < TILES:
+                clamp(before, 1)
+                send_on_gpsimd(before, 1)
+            operands = []
+            if 0 <= late < TILES:
+                turn_sent(late)
+                operands.append(("b", late))
+            if ahead < TILES:
+                turn_emission(ahead)
+                operands.append(("e", ahead))
+            if operands:
+                group(step, operands)
+            if step == 0:
+                for g in range(PASSES):
+                    sort_rho(0, g)
+            if SORT_E and step + 2 < TILES:
+                sort_emission(step + 2)
+            if 0 <= before < TILES:
+                for half in range(PASSES):
+                    send_on_vector(before, half)
+            if step < TILES:
+                bounce("e", step, direct)
+                add_ambient(step, 0)
+                clamp(step, 0)
+            next_room, place = divmod(step + 1, TILES_PER_ROOM)
+            if 0 < next_room < ROOMS and place < PASSES:
+                sort_rho(next_room, place)
+            if operands:
+                quantize(step, operands)
+            if step < TILES:
+                send_on_gpsimd(step, 0)
+                add_ambient(step, 1)
+            if last >= 0:
+                bounce("b", last, second)
+                finish(last)

@@ -18,15 +18,20 @@ ACT = mybir.ActivationFunctionType
 
 P = 128
 HALF = 512
+RUN = 256
 PASSES = PATCHES // HALF
 TILES_PER_ROOM = STATES // P
 TILES = ROOMS * TILES_PER_ROOM
-LAG_T = 2
-LAG_M = 3
-SHARE = 4
-SHARE_FIRST = 4
-N_FIRST = 1
-SHARE_LAST = 2
+LOAD_AHEAD = 5
+LAG = 3
+GPSIMD_COLUMNS = 640
+C0 = 0
+C1 = 640
+C2 = 640
+C13 = 640
+C14 = 256
+C15 = 0
+TAIL = 0
 SORT_E = 0
 
 
@@ -51,20 +56,23 @@ def tile_two_bounce_signed_transfer_s14_kernel(tc, emission, ff_words, ff_scales
         first_scales = sbuf.tile([P, PASSES * PATCHES], U8, name="first_scales", align_bytes=64)
         later_scales = sbuf.tile([P, (ROOMS - 1) * PASSES * PATCHES], U8, name="later_scales", align_bytes=64)
         nc.vector.memset(first_scales[:].bitcast(I32), 0)
-        nc.vector.memset(later_scales[:].bitcast(I32), 0)
+        nc.gpsimd.memset(later_scales[:].bitcast(I32), 0)
 
         emitted, weights, ambient_rows, rho_rows, rho_sorted = {}, {}, {}, {}, {}
         received, clamped, sent, turned, codes, scales = {}, {}, {}, {}, {}, {}
-        direct, second, ordered, grouped = {}, {}, {}, {}
+        direct, second, ordered, grouped, members = {}, {}, {}, {}, {}
 
         def load_emission(i):
             room, row = divmod(i, TILES_PER_ROOM)
             emitted[i] = slot(sbuf, "emitted", i, TILES, [P, PATCHES], BF16)
             nc.sync.dma_start(out=emitted[i][:], in_=emission[room, row * P:(row + 1) * P, :])
 
-        def load_weights(group):
-            weights[group] = slot(sbuf, "weights", group, ROOMS * PASSES, [P, 2 * PATCHES], U8)
-            nc.sync.dma_start(out=weights[group][:].bitcast(I32), in_=ff_words[group].bitcast(I32))
+        def load_weights(room):
+            weights[room] = slot(sbuf, "weights", room, ROOMS, [P, PASSES * 2 * PATCHES], U8)
+            nc.sync.dma_start(
+                out=weights[room][:].bitcast(I32).rearrange("p (g n) -> p g n", g=PASSES),
+                in_=ff_words[room * PASSES:(room + 1) * PASSES].bitcast(I32).rearrange("g p n -> p g n"),
+            )
 
         def load_scales(plane, first_group, groups):
             for quadrant in range(4):
@@ -75,19 +83,8 @@ def tile_two_bounce_signed_transfer_s14_kernel(tc, emission, ff_words, ff_scales
                 )
 
         def load_row(store, kind, source, room):
-            store[room] = slot(sbuf, kind, room, ROOMS, [P, PATCHES], BF16)
+            store[room] = slot(sbuf, kind, room, 2, [P, PATCHES], BF16)
             nc.sync.dma_start(out=store[room][:], in_=source[room].partition_broadcast(P))
-
-        def load_room(room):
-            first = room * TILES_PER_ROOM
-            load_emission(first)
-            for g in range(PASSES):
-                load_weights(room * PASSES + g)
-            load_row(ambient_rows, "ambient", ambient, room)
-            load_emission(first + 1)
-            load_row(rho_rows, "rho", rho, room)
-            for i in range(first + 2, first + TILES_PER_ROOM):
-                load_emission(i)
 
         def weight_scales(room, g, half):
             if room == 0:
@@ -97,10 +94,12 @@ def tile_two_bounce_signed_transfer_s14_kernel(tc, emission, ff_words, ff_scales
             return plane[:, start + half * HALF:start + (half + 1) * HALF]
 
         def sort_rho(room, g):
-            rho_sorted[room, g] = slot(sbuf, "rho_sorted", PASSES * room + g, 2 * PASSES, [P, HALF], F32)
+            if g == 0:
+                rho_sorted[room] = slot(sbuf, "rho_sorted", room, 2, [P, PATCHES], F32)
+            cols = slice(g * HALF, (g + 1) * HALF)
             nc.scalar.copy(
-                out=rho_sorted[room, g][:].rearrange("p (u m e) -> p u m e", u=2, e=2),
-                in_=rho_rows[room][:, g * HALF:(g + 1) * HALF].rearrange("p (m u e) -> p u m e", u=2, e=2),
+                out=rho_sorted[room][:, cols].rearrange("p (u m e) -> p u m e", u=2, e=2),
+                in_=rho_rows[room][:, cols].rearrange("p (m u e) -> p u m e", u=2, e=2),
             )
 
         def sort_emission(i):
@@ -124,44 +123,33 @@ def tile_two_bounce_signed_transfer_s14_kernel(tc, emission, ff_words, ff_scales
 
         def turn_sent(i):
             turned["b", i] = bank("turned", len(turned), 2)
-            for g in range(PASSES):
-                words = sent[i, g][:].bitcast(F32)
-                for u in range(2):
-                    nc.tensor.transpose(
-                        turned["b", i][:, (2 * g + u) * P:(2 * g + u + 1) * P],
-                        words[:, u * P:(u + 1) * P],
-                        identity[:],
-                    )
+            words = sent[i][:].bitcast(F32)
+            for run in range(2 * PASSES):
+                cols = slice(run * P, (run + 1) * P)
+                nc.tensor.transpose(turned["b", i][:, cols], words[:, cols], identity[:])
 
-        def group(step, operands):
-            grouped[step] = slot(sbuf, "grouped", step, 2, [P, 2 * PATCHES], BF16)
-            for n, key in enumerate(operands):
-                nc.scalar.copy(
-                    out=grouped[step][:, n * PATCHES:(n + 1) * PATCHES].bitcast(F32).rearrange("p (g s u) -> p g s u", g=PASSES, u=2),
-                    in_=turned[key][:].rearrange("p (g u s) -> p g s u", g=PASSES, u=2),
-                )
-
-        def quantize(step, operands):
-            width = len(operands) * PASSES * P
-            step_codes = slot(sbuf, "codes", step, 3, [P, 2 * PASSES * P], U32)
-            step_scales = slot(sbuf, "scales", step, 3, [P, 2 * PASSES * P], U8)
-            for n, key in enumerate(operands):
-                codes[key] = step_codes[:, n * PASSES * P:(n + 1) * PASSES * P]
-                scales[key] = step_scales[:, n * PASSES * P:(n + 1) * PASSES * P]
-            nc.vector.quantize_mx(
-                out=step_codes[:, :width].bitcast(FP8X4), scales=step_scales[:, :width], in_=grouped[step][:, :4 * width]
+        def group(key):
+            grouped[key] = slot(sbuf, "grouped_" + key[0], key[1], 2, [P, PATCHES], BF16)
+            nc.scalar.copy(
+                out=grouped[key][:].bitcast(F32).rearrange("p (g s u) -> p g s u", g=PASSES, u=2),
+                in_=turned[key][:].rearrange("p (g u s) -> p g s u", g=PASSES, u=2),
             )
+
+        def quantize(key):
+            codes[key] = slot(sbuf, "codes_" + key[0], key[1], 3, [P, PASSES * P], U32)
+            scales[key] = slot(sbuf, "scales_" + key[0], key[1], 3, [P, PASSES * P], U8)
+            nc.vector.quantize_mx(out=codes[key][:].bitcast(FP8X4), scales=scales[key][:], in_=grouped[key][:])
 
         def bounce(kind, i, sums):
             room = i // TILES_PER_ROOM
             for half in range(PASSES):
-                sums[i, half] = bank("sums_" + kind, PASSES * i + half, 3)
+                sums[i, half] = bank("sums", len(direct) + len(second), 6)
                 for g in range(PASSES):
                     nc.tensor.matmul_mx(
                         out=sums[i, half][:],
                         lhsT=codes[kind, i][:, g * P:(g + 1) * P].bitcast(FP8X4),
                         lhsT_scale=scales[kind, i][:, g * P:(g + 1) * P],
-                        rhs=weights[room * PASSES + g][:, 2 * half * HALF:2 * (half + 1) * HALF].bitcast(FP4X4),
+                        rhs=weights[room][:, 2 * (g * PATCHES + half * HALF):2 * (g * PATCHES + (half + 1) * HALF)].bitcast(FP4X4),
                         rhs_scale=weight_scales(room, g, half),
                         start=(g == 0),
                         stop=(g == PASSES - 1),
@@ -169,58 +157,69 @@ def tile_two_bounce_signed_transfer_s14_kernel(tc, emission, ff_words, ff_scales
 
         def add_ambient(i, half):
             room = i // TILES_PER_ROOM
-            received[i, half] = slot(sbuf, "received", PASSES * i + half, PASSES * (LAG_M + 2), [P, HALF], F32)
+            received[i, half] = slot(sbuf, "received", PASSES * i + half, PASSES * (LAG + 2), [P, HALF], F32)
             nc.vector.tensor_tensor(
                 out=received[i, half][:],
                 in0=ambient_rows[room][:, half * HALF:(half + 1) * HALF],
                 in1=direct[i, half][:],
                 op=ALU.add,
             )
-            sent[i, half] = slot(sbuf, "sent", PASSES * i + half, 6, [P, HALF], BF16)
 
-        def gpsimd_runs(i, half):
-            quarters = SHARE_FIRST if i < N_FIRST else SHARE_LAST if i == TILES - 1 else SHARE
-            return max(0, min(2, quarters - 2 * half))
+        def runs(start, stop):
+            edges = [start] + [c for c in range(RUN, PATCHES, RUN) if start < c < stop] + [stop]
+            return [(a, b) for a, b in zip(edges, edges[1:]) if a < b]
 
-        def send_on_vector(i, half):
-            room = i // TILES_PER_ROOM
-            pairs = received[i, half][:].rearrange("p (m u e) -> p u m e", u=2, e=2)
-            for u in range(gpsimd_runs(i, half), 2):
-                cols = slice(u * 2 * P, (u + 1) * 2 * P)
+        def pairs(i, a, b):
+            half, u = divmod(a // RUN, 2)
+            view = received[i, half][:].rearrange("p (m u e) -> p u m e", u=2, e=2)
+            return view[:, u, (a % RUN) // 2:(a % RUN + b - a) // 2, :]
+
+        def clamp(i, half):
+            stop = min(split(i), (half + 1) * HALF)
+            if stop <= half * HALF:
+                return
+            if i not in clamped:
+                clamped[i] = slot(sbuf, "clamped", i, 2, [P, PATCHES], F32)
+            if stop == (half + 1) * HALF:
+                nc.scalar.activation(
+                    out=clamped[i][:, half * HALF:stop].rearrange("p (u m e) -> p u m e", u=2, e=2),
+                    in_=received[i, half][:].rearrange("p (m u e) -> p u m e", u=2, e=2),
+                    func=ACT.Relu,
+                )
+            else:
+                for a, b in runs(half * HALF, stop):
+                    nc.scalar.activation(
+                        out=clamped[i][:, a:b].rearrange("p (m e) -> p m e", e=2), in_=pairs(i, a, b), func=ACT.Relu
+                    )
+
+        def send_on_gpsimd(i):
+            cols = slice(0, split(i))
+            if split(i) > 0:
+                nc.gpsimd.tensor_tensor(
+                    out=sent[i][:, cols],
+                    in0=clamped[i][:, cols],
+                    in1=rho_sorted[i // TILES_PER_ROOM][:, cols],
+                    op=ALU.mult,
+                )
+
+        def send_on_vector(i):
+            sent[i] = slot(sbuf, "sent", i, 3, [P, PATCHES], BF16)
+            for a, b in runs(split(i), PATCHES):
                 nc.vector.scalar_tensor_tensor(
-                    out=sent[i, half][:, cols].rearrange("p (m e) -> p m e", e=2),
-                    in0=pairs[:, u],
+                    out=sent[i][:, a:b].rearrange("p (m e) -> p m e", e=2),
+                    in0=pairs(i, a, b),
                     scalar=0.0,
-                    in1=rho_sorted[room, half][:, cols].rearrange("p (m e) -> p m e", e=2),
+                    in1=rho_sorted[i // TILES_PER_ROOM][:, a:b].rearrange("p (m e) -> p m e", e=2),
                     op0=ALU.max,
                     op1=ALU.mult,
                 )
 
-        def clamp(i, half):
-            runs = gpsimd_runs(i, half)
-            if runs > 0:
-                pairs = received[i, half][:].rearrange("p (m u e) -> p u m e", u=2, e=2)
-                clamped[i, half] = slot(sbuf, "clamped", PASSES * i + half, 4, [P, HALF], F32)
-                nc.scalar.activation(
-                    out=clamped[i, half][:, :runs * 2 * P].rearrange("p (u m e) -> p u m e", u=runs, e=2),
-                    in_=pairs[:, :runs],
-                    func=ACT.Relu,
-                )
+        def split(i):
+            return {0: C0, 1: C1, 2: C2, 13: C13, 14: C14, 15: C15}.get(i, GPSIMD_COLUMNS)
 
-        def send_on_gpsimd(i, half):
-            room = i // TILES_PER_ROOM
-            width = gpsimd_runs(i, half) * 2 * P
-            if width > 0:
-                nc.gpsimd.tensor_tensor(
-                    out=sent[i, half][:, :width],
-                    in0=clamped[i, half][:, :width],
-                    in1=rho_sorted[room, half][:, :width],
-                    op=ALU.mult,
-                )
-
-        def finish(i):
+        def finish(i, halves=(0, 1)):
             room, row = divmod(i, TILES_PER_ROOM)
-            for half in range(PASSES):
+            for half in halves:
                 result = slot(sbuf, "result", PASSES * i + half, 8, [P, HALF], F32)
                 nc.vector.scalar_tensor_tensor(
                     out=result[:],
@@ -237,53 +236,114 @@ def tile_two_bounce_signed_transfer_s14_kernel(tc, emission, ff_words, ff_scales
         load_emission(0)
         load_emission(1)
         load_scales(first_scales, 0, PASSES)
-        for g in range(PASSES):
-            load_weights(g)
+        load_weights(0)
         load_row(ambient_rows, "ambient", ambient, 0)
         load_emission(2)
         load_row(rho_rows, "rho", rho, 0)
-        load_emission(3)
+        for i in range(3, LOAD_AHEAD):
+            load_emission(i)
         load_scales(later_scales, PASSES, (ROOMS - 1) * PASSES)
-        for room in range(1, ROOMS):
-            load_room(room)
 
-        turn_emission(0)
-        group(-1, [("e", 0)])
-        quantize(-1, [("e", 0)])
-        for step in range(TILES + LAG_M):
-            ahead, before, late, last = step + 1, step - 1, step - LAG_T, step - LAG_M
-            if 0 <= before < TILES:
-                clamp(before, 1)
-                send_on_gpsimd(before, 1)
-            operands = []
-            if 0 <= late < TILES:
-                turn_sent(late)
-                operands.append(("b", late))
-            if ahead < TILES:
-                turn_emission(ahead)
-                operands.append(("e", ahead))
-            if operands:
-                group(step, operands)
+        for i in range(2):
+            turn_emission(i)
+            group(("e", i))
+        quantize(("e", 0))
+        for step in range(TILES):
+            ahead, before, late = step + 2, step - 1, step - LAG
+            room, place = divmod(step, TILES_PER_ROOM)
+            if step + LOAD_AHEAD < TILES:
+                load_emission(step + LOAD_AHEAD)
+            if room + 1 < ROOMS and place == 0:
+                load_weights(room + 1)
+            if room + 1 < ROOMS and place == 1:
+                load_row(rho_rows, "rho", rho, room + 1)
+            if room + 1 < ROOMS and place == 2:
+                load_row(ambient_rows, "ambient", ambient, room + 1)
             if step == 0:
                 for g in range(PASSES):
                     sort_rho(0, g)
-            if SORT_E and step + 2 < TILES:
-                sort_emission(step + 2)
-            if 0 <= before < TILES:
-                for half in range(PASSES):
-                    send_on_vector(before, half)
-            if step < TILES:
                 bounce("e", step, direct)
-                add_ambient(step, 0)
-                clamp(step, 0)
-            next_room, place = divmod(step + 1, TILES_PER_ROOM)
-            if 0 < next_room < ROOMS and place < PASSES:
-                sort_rho(next_room, place)
-            if operands:
-                quantize(step, operands)
-            if step < TILES:
-                send_on_gpsimd(step, 0)
-                add_ambient(step, 1)
-            if last >= 0:
-                bounce("b", last, second)
-                finish(last)
+            if late >= 0:
+                turn_sent(late)
+                group(("b", late))
+            if ahead < TILES:
+                turn_emission(ahead)
+            if before >= 0:
+                send_on_vector(before)
+                clamp(before, 0)
+            if step + 1 < TILES:
+                quantize(("e", step + 1))
+            if late >= 0:
+                quantize(("b", late))
+            if before >= 0:
+                send_on_gpsimd(before)
+            if ahead < TILES:
+                group(("e", ahead))
+            if SORT_E and step + 3 < TILES:
+                sort_emission(step + 3)
+            if step > 0:
+                bounce("e", step, direct)
+            for half in range(PASSES):
+                add_ambient(step, half)
+            clamp(step, 1)
+            if place >= TILES_PER_ROOM - PASSES and room + 1 < ROOMS:
+                sort_rho(room + 1, place - (TILES_PER_ROOM - PASSES))
+            if step == TILES - 1:
+                break
+            if late >= 0:
+                bounce("b", late, second)
+                finish(late)
+        turn_sent(13)
+        group(("b", 13))
+        bounce("b", 12, second)
+        if TAIL == 0:
+            quantize(("b", 13))
+            send_on_vector(15)
+            turn_sent(14)
+            group(("b", 14))
+            bounce("b", 13, second)
+            turn_sent(15)
+            group(("b", 15))
+            finish(12)
+            quantize(("b", 14))
+            bounce("b", 14, second)
+            finish(13)
+            quantize(("b", 15))
+            bounce("b", 15, second)
+            finish(14)
+            finish(15)
+        elif TAIL == 1:
+            send_on_vector(15)
+            quantize(("b", 13))
+            turn_sent(14)
+            group(("b", 14))
+            turn_sent(15)
+            group(("b", 15))
+            bounce("b", 13, second)
+            quantize(("b", 14))
+            finish(12)
+            quantize(("b", 15))
+            bounce("b", 14, second)
+            bounce("b", 15, second)
+            finish(13)
+            finish(14)
+            finish(15)
+        else:
+            quantize(("b", 13))
+            send_on_vector(15)
+            turn_sent(14)
+            group(("b", 14))
+            clamp(15, 0)
+            send_on_gpsimd(15)
+            bounce("b", 13, second)
+            finish(12)
+            finish(13, (0,))
+            quantize(("b", 14))
+            turn_sent(15)
+            group(("b", 15))
+            bounce("b", 14, second)
+            finish(13, (1,))
+            quantize(("b", 15))
+            bounce("b", 15, second)
+            finish(14)
+            finish(15)

@@ -17,22 +17,17 @@ ALU = mybir.AluOpType
 ACT = mybir.ActivationFunctionType
 
 P = 128
-HALF = 512
-RUN = 256
-PASSES = PATCHES // HALF
+GROUP = 512
+GROUPS = PATCHES // GROUP
 TILES_PER_ROOM = STATES // P
 TILES = ROOMS * TILES_PER_ROOM
+QUADRANTS = 4
+
 LOAD_AHEAD = 5
+TURN_DISTANCE = 2
 LAG = 3
-GPSIMD_COLUMNS = 640
-C0 = 0
-C1 = 640
-C2 = 640
-C13 = 640
-C14 = 256
-C15 = 0
-TAIL = 0
-SORT_E = 0
+SUM_BANKS = 6
+TURN_BANKS = 2
 
 
 def tile_two_bounce_signed_transfer_s14_kernel(tc, emission, ff_words, ff_scales, ambient, rho, out):
@@ -42,308 +37,228 @@ def tile_two_bounce_signed_transfer_s14_kernel(tc, emission, ff_words, ff_scales
         psum = ctx.enter_context(tc.psum_pool(name="psum", bufs=1))
         ctx.enter_context(tc.manual_schedule())
 
-        def slot(pool, kind, index, slots, shape, dtype):
+        def slot(kind, index, slots, shape, dtype):
             name = "%s%d" % (kind, index % slots)
-            return pool.tile(shape, dtype, name=name, tag=name, align_bytes=64)
+            return sbuf.tile(shape, dtype, name=name, tag=name, align_bytes=64)
 
-        def bank(kind, index, slots):
-            name = "%s%d" % (kind, index % slots)
-            return psum.tile([P, HALF], F32, name=name, tag=name)
+        def bank(kind, index, banks):
+            name = "%s%d" % (kind, index % banks)
+            return psum.tile([P, GROUP], F32, name=name, tag=name)
 
         identity = sbuf.tile([P, P], F32, name="identity", align_bytes=64)
         make_identity(nc, identity[:])
 
-        first_scales = sbuf.tile([P, PASSES * PATCHES], U8, name="first_scales", align_bytes=64)
-        later_scales = sbuf.tile([P, (ROOMS - 1) * PASSES * PATCHES], U8, name="later_scales", align_bytes=64)
+        first_scales = sbuf.tile([P, GROUPS * PATCHES], U8, name="first_scales", align_bytes=64)
+        later_scales = sbuf.tile([P, (ROOMS - 1) * GROUPS * PATCHES], U8, name="later_scales", align_bytes=64)
         nc.vector.memset(first_scales[:].bitcast(I32), 0)
         nc.gpsimd.memset(later_scales[:].bitcast(I32), 0)
 
-        emitted, weights, ambient_rows, rho_rows, rho_sorted = {}, {}, {}, {}, {}
-        received, clamped, sent, turned, codes, scales = {}, {}, {}, {}, {}, {}
-        direct, second, ordered, grouped, members = {}, {}, {}, {}, {}
+        emitted, ordered, weights, ambient_rows, rho_rows = {}, {}, {}, {}, {}
+        turned, staged, codes, scales = {}, {}, {}, {}
+        direct, received, clamped, sent, second = {}, {}, {}, {}, {}
 
         def load_emission(i):
             room, row = divmod(i, TILES_PER_ROOM)
-            emitted[i] = slot(sbuf, "emitted", i, TILES, [P, PATCHES], BF16)
+            emitted[i] = slot("emitted", i, TILES, [P, PATCHES], BF16)
             nc.sync.dma_start(out=emitted[i][:], in_=emission[room, row * P:(row + 1) * P, :])
 
         def load_weights(room):
-            weights[room] = slot(sbuf, "weights", room, ROOMS, [P, PASSES * 2 * PATCHES], U8)
+            weights[room] = slot("weights", room, ROOMS, [P, GROUPS * 2 * PATCHES], U8)
             nc.sync.dma_start(
-                out=weights[room][:].bitcast(I32).rearrange("p (g n) -> p g n", g=PASSES),
-                in_=ff_words[room * PASSES:(room + 1) * PASSES].bitcast(I32).rearrange("g p n -> p g n"),
+                out=weights[room][:].bitcast(I32).rearrange("p (g n) -> p g n", g=GROUPS),
+                in_=ff_words[room * GROUPS:(room + 1) * GROUPS].bitcast(I32).rearrange("g p n -> p g n"),
             )
 
         def load_scales(plane, first_group, groups):
-            for quadrant in range(4):
+            for quadrant in range(QUADRANTS):
                 nc.sync.dma_start(
                     out=plane[32 * quadrant:32 * quadrant + 4, :].bitcast(I32).rearrange("q (g n) -> q g n", g=groups),
                     in_=ff_scales[first_group:first_group + groups, 4 * quadrant:4 * quadrant + 4, :]
                     .bitcast(I32).rearrange("g q n -> q g n"),
                 )
 
-        def load_row(store, kind, source, room):
-            store[room] = slot(sbuf, kind, room, 2, [P, PATCHES], BF16)
-            nc.sync.dma_start(out=store[room][:], in_=source[room].partition_broadcast(P))
+        def load_row(rows, kind, source, room):
+            rows[room] = slot(kind, room, 2, [P, PATCHES], BF16)
+            nc.sync.dma_start(out=rows[room][:], in_=source[room].partition_broadcast(P))
 
         def weight_scales(room, g, half):
             if room == 0:
                 plane, start = first_scales, g * PATCHES
             else:
-                plane, start = later_scales, ((room - 1) * PASSES + g) * PATCHES
-            return plane[:, start + half * HALF:start + (half + 1) * HALF]
+                plane, start = later_scales, ((room - 1) * GROUPS + g) * PATCHES
+            return plane[:, start + half * GROUP:start + (half + 1) * GROUP]
 
-        def sort_rho(room, g):
-            if g == 0:
-                rho_sorted[room] = slot(sbuf, "rho_sorted", room, 2, [P, PATCHES], F32)
-            cols = slice(g * HALF, (g + 1) * HALF)
-            nc.scalar.copy(
-                out=rho_sorted[room][:, cols].rearrange("p (u m e) -> p u m e", u=2, e=2),
-                in_=rho_rows[room][:, cols].rearrange("p (m u e) -> p u m e", u=2, e=2),
-            )
+        def even_and_odd(groups):
+            return [values.bitcast(F32)[:, odd::2] for values in groups for odd in range(2)]
+
+        def turn(operand, quarters):
+            turned[operand] = bank("turned", len(turned), TURN_BANKS)
+            for n, words in enumerate(quarters):
+                nc.tensor.transpose(turned[operand][:, n * P:(n + 1) * P], words, identity[:])
 
         def sort_emission(i):
-            ordered[i] = slot(sbuf, "ordered", i, 2, [P, HALF], F32)
+            ordered[i] = slot("ordered", i, 2, [P, GROUP], F32)
             nc.scalar.copy(
-                out=ordered[i][:].rearrange("p (g u m) -> p g u m", g=PASSES, u=2),
-                in_=emitted[i][:].bitcast(F32).rearrange("p (g m u) -> p g u m", g=PASSES, u=2),
+                out=ordered[i][:].rearrange("p (g u m) -> p g u m", g=GROUPS, u=2),
+                in_=emitted[i][:].bitcast(F32).rearrange("p (g m u) -> p g u m", g=GROUPS, u=2),
             )
 
         def turn_emission(i):
-            turned["e", i] = bank("turned", len(turned), 2)
-            words = emitted[i][:].bitcast(F32)
-            for g in range(PASSES):
-                for u in range(2):
-                    nc.tensor.transpose(
-                        turned["e", i][:, (2 * g + u) * P:(2 * g + u + 1) * P],
-                        ordered[i][:, (2 * g + u) * P:(2 * g + u + 1) * P] if i in ordered
-                        else words[:, 2 * P * g + u:2 * P * (g + 1):2],
-                        identity[:],
-                    )
+            if i in ordered:
+                turn(("e", i), [ordered[i][:, n * P:(n + 1) * P] for n in range(2 * GROUPS)])
+            else:
+                turn(("e", i), even_and_odd([emitted[i][:, g * GROUP:(g + 1) * GROUP] for g in range(GROUPS)]))
 
         def turn_sent(i):
-            turned["b", i] = bank("turned", len(turned), 2)
-            words = sent[i][:].bitcast(F32)
-            for run in range(2 * PASSES):
-                cols = slice(run * P, (run + 1) * P)
-                nc.tensor.transpose(turned["b", i][:, cols], words[:, cols], identity[:])
+            turn(("b", i), even_and_odd([sent[i, g] for g in range(GROUPS)]))
 
-        def group(key):
-            grouped[key] = slot(sbuf, "grouped_" + key[0], key[1], 2, [P, PATCHES], BF16)
+        def staging(operand):
+            return slot("staged_" + operand[0], operand[1], 2, [P, PATCHES], BF16)
+
+        def stage(operand):
+            staged[operand] = staging(operand)
             nc.scalar.copy(
-                out=grouped[key][:].bitcast(F32).rearrange("p (g s u) -> p g s u", g=PASSES, u=2),
-                in_=turned[key][:].rearrange("p (g u s) -> p g s u", g=PASSES, u=2),
+                out=staged[operand][:].bitcast(F32).rearrange("p (g s u) -> p g s u", g=GROUPS, u=2),
+                in_=turned[operand][:].rearrange("p (g u s) -> p g s u", g=GROUPS, u=2),
             )
 
-        def quantize(key):
-            codes[key] = slot(sbuf, "codes_" + key[0], key[1], 3, [P, PASSES * P], U32)
-            scales[key] = slot(sbuf, "scales_" + key[0], key[1], 3, [P, PASSES * P], U8)
-            nc.vector.quantize_mx(out=codes[key][:].bitcast(FP8X4), scales=scales[key][:], in_=grouped[key][:])
+        def quantize(operand):
+            kind, i = operand
+            codes[operand] = slot("codes_" + kind, i, 3, [P, GROUPS * P], U32)
+            scales[operand] = slot("scales_" + kind, i, 3, [P, GROUPS * P], U8)
+            nc.vector.quantize_mx(
+                out=codes[operand][:].bitcast(FP8X4), scales=scales[operand][:], in_=staged[operand][:]
+            )
 
-        def bounce(kind, i, sums):
+        def bounce(operand, sums):
+            i = operand[1]
             room = i // TILES_PER_ROOM
-            for half in range(PASSES):
-                sums[i, half] = bank("sums", len(direct) + len(second), 6)
-                for g in range(PASSES):
+            for half in range(GROUPS):
+                sums[i, half] = bank("sums", len(direct) + len(second), SUM_BANKS)
+                for g in range(GROUPS):
+                    column = g * PATCHES + half * GROUP
                     nc.tensor.matmul_mx(
                         out=sums[i, half][:],
-                        lhsT=codes[kind, i][:, g * P:(g + 1) * P].bitcast(FP8X4),
-                        lhsT_scale=scales[kind, i][:, g * P:(g + 1) * P],
-                        rhs=weights[room][:, 2 * (g * PATCHES + half * HALF):2 * (g * PATCHES + (half + 1) * HALF)].bitcast(FP4X4),
+                        lhsT=codes[operand][:, g * P:(g + 1) * P].bitcast(FP8X4),
+                        lhsT_scale=scales[operand][:, g * P:(g + 1) * P],
+                        rhs=weights[room][:, 2 * column:2 * (column + GROUP)].bitcast(FP4X4),
                         rhs_scale=weight_scales(room, g, half),
                         start=(g == 0),
-                        stop=(g == PASSES - 1),
+                        stop=(g == GROUPS - 1),
                     )
 
         def add_ambient(i, half):
-            room = i // TILES_PER_ROOM
-            received[i, half] = slot(sbuf, "received", PASSES * i + half, PASSES * (LAG + 2), [P, HALF], F32)
+            received[i, half] = slot("received", GROUPS * i + half, 2 * GROUPS, [P, GROUP], F32)
             nc.vector.tensor_tensor(
                 out=received[i, half][:],
-                in0=ambient_rows[room][:, half * HALF:(half + 1) * HALF],
+                in0=ambient_rows[i // TILES_PER_ROOM][:, half * GROUP:(half + 1) * GROUP],
                 in1=direct[i, half][:],
                 op=ALU.add,
             )
 
-        def runs(start, stop):
-            edges = [start] + [c for c in range(RUN, PATCHES, RUN) if start < c < stop] + [stop]
-            return [(a, b) for a, b in zip(edges, edges[1:]) if a < b]
-
-        def pairs(i, a, b):
-            half, u = divmod(a // RUN, 2)
-            view = received[i, half][:].rearrange("p (m u e) -> p u m e", u=2, e=2)
-            return view[:, u, (a % RUN) // 2:(a % RUN + b - a) // 2, :]
-
         def clamp(i, half):
-            stop = min(split(i), (half + 1) * HALF)
-            if stop <= half * HALF:
-                return
-            if i not in clamped:
-                clamped[i] = slot(sbuf, "clamped", i, 2, [P, PATCHES], F32)
-            if stop == (half + 1) * HALF:
-                nc.scalar.activation(
-                    out=clamped[i][:, half * HALF:stop].rearrange("p (u m e) -> p u m e", u=2, e=2),
-                    in_=received[i, half][:].rearrange("p (m u e) -> p u m e", u=2, e=2),
-                    func=ACT.Relu,
-                )
-            else:
-                for a, b in runs(half * HALF, stop):
-                    nc.scalar.activation(
-                        out=clamped[i][:, a:b].rearrange("p (m e) -> p m e", e=2), in_=pairs(i, a, b), func=ACT.Relu
-                    )
+            clamped[i, half] = slot("clamped", GROUPS * i + half, GROUPS * (LAG + 2), [P, GROUP], F32)
+            nc.scalar.activation(out=clamped[i, half][:], in_=received[i, half][:], func=ACT.Relu)
 
-        def send_on_gpsimd(i):
-            cols = slice(0, split(i))
-            if split(i) > 0:
-                nc.gpsimd.tensor_tensor(
-                    out=sent[i][:, cols],
-                    in0=clamped[i][:, cols],
-                    in1=rho_sorted[i // TILES_PER_ROOM][:, cols],
-                    op=ALU.mult,
-                )
+        def send(engine, i, half):
+            engine.tensor_tensor(
+                out=sent[i, half],
+                in0=clamped[i, half][:],
+                in1=rho_rows[i // TILES_PER_ROOM][:, half * GROUP:(half + 1) * GROUP],
+                op=ALU.mult,
+            )
 
-        def send_on_vector(i):
-            sent[i] = slot(sbuf, "sent", i, 3, [P, PATCHES], BF16)
-            for a, b in runs(split(i), PATCHES):
-                nc.vector.scalar_tensor_tensor(
-                    out=sent[i][:, a:b].rearrange("p (m e) -> p m e", e=2),
-                    in0=pairs(i, a, b),
-                    scalar=0.0,
-                    in1=rho_sorted[i // TILES_PER_ROOM][:, a:b].rearrange("p (m e) -> p m e", e=2),
-                    op0=ALU.max,
-                    op1=ALU.mult,
-                )
+        def send_on_vector(i, half):
+            sent[i, half] = slot("sent", i + half, 3, [P, GROUP], BF16)[:, :]
+            send(nc.vector, i, half)
 
-        def split(i):
-            return {0: C0, 1: C1, 2: C2, 13: C13, 14: C14, 15: C15}.get(i, GPSIMD_COLUMNS)
+        def send_on_gpsimd(i, consumed):
+            sent[i, 1] = staging(consumed)[:, :GROUP]
+            send(nc.gpsimd, i, 1)
 
-        def finish(i, halves=(0, 1)):
+        def finish(i):
             room, row = divmod(i, TILES_PER_ROOM)
-            for half in halves:
-                result = slot(sbuf, "result", PASSES * i + half, 8, [P, HALF], F32)
-                nc.vector.scalar_tensor_tensor(
-                    out=result[:],
-                    in0=received[i, half][:],
-                    scalar=0.0,
-                    in1=second[i, half][:],
-                    op0=ALU.max,
-                    op1=ALU.add,
-                )
+            for half in range(GROUPS):
+                result = slot("result", GROUPS * i + half, GROUPS * TILES, [P, GROUP], F32)
+                nc.vector.tensor_tensor(out=result[:], in0=clamped[i, half][:], in1=second[i, half][:], op=ALU.add)
                 nc.sync.dma_start(
-                    out=out[room, row * P:(row + 1) * P, half * HALF:(half + 1) * HALF], in_=result[:]
+                    out=out[room, row * P:(row + 1) * P, half * GROUP:(half + 1) * GROUP], in_=result[:]
                 )
 
         load_emission(0)
         load_emission(1)
-        load_scales(first_scales, 0, PASSES)
+        load_scales(first_scales, 0, GROUPS)
         load_weights(0)
         load_row(ambient_rows, "ambient", ambient, 0)
         load_emission(2)
         load_row(rho_rows, "rho", rho, 0)
         for i in range(3, LOAD_AHEAD):
             load_emission(i)
-        load_scales(later_scales, PASSES, (ROOMS - 1) * PASSES)
+        load_scales(later_scales, GROUPS, (ROOMS - 1) * GROUPS)
 
-        for i in range(2):
+        for i in range(TURN_DISTANCE):
             turn_emission(i)
-            group(("e", i))
+            stage(("e", i))
         quantize(("e", 0))
+        bounce(("e", 0), direct)
+
         for step in range(TILES):
-            ahead, before, late = step + 2, step - 1, step - LAG
             room, place = divmod(step, TILES_PER_ROOM)
+            ahead, behind, late = step + TURN_DISTANCE, step - TURN_DISTANCE, step - LAG
             if step + LOAD_AHEAD < TILES:
                 load_emission(step + LOAD_AHEAD)
             if room + 1 < ROOMS and place == 0:
                 load_weights(room + 1)
             if room + 1 < ROOMS and place == 1:
-                load_row(rho_rows, "rho", rho, room + 1)
-            if room + 1 < ROOMS and place == 2:
                 load_row(ambient_rows, "ambient", ambient, room + 1)
-            if step == 0:
-                for g in range(PASSES):
-                    sort_rho(0, g)
-                bounce("e", step, direct)
-            if late >= 0:
-                turn_sent(late)
-                group(("b", late))
+            if room + 1 < ROOMS and place == 2:
+                load_row(rho_rows, "rho", rho, room + 1)
+
+            if step >= 1:
+                send_on_vector(step - 1, 0)
+            operands = [("b", late)] if late >= 0 else []
+            if step + 1 < TILES:
+                operands.append(("e", step + 1))
+            for operand in operands:
+                quantize(operand)
+            if step >= 1:
+                send_on_gpsimd(step - 1, operands[-1])
+
+            if behind >= 0:
+                turn_sent(behind)
             if ahead < TILES:
                 turn_emission(ahead)
-            if before >= 0:
-                send_on_vector(before)
-                clamp(before, 0)
-            if step + 1 < TILES:
-                quantize(("e", step + 1))
-            if late >= 0:
-                quantize(("b", late))
-            if before >= 0:
-                send_on_gpsimd(before)
-            if ahead < TILES:
-                group(("e", ahead))
-            if SORT_E and step + 3 < TILES:
-                sort_emission(step + 3)
-            if step > 0:
-                bounce("e", step, direct)
-            for half in range(PASSES):
+            for half in range(GROUPS):
                 add_ambient(step, half)
-            clamp(step, 1)
-            if place >= TILES_PER_ROOM - PASSES and room + 1 < ROOMS:
-                sort_rho(room + 1, place - (TILES_PER_ROOM - PASSES))
-            if step == TILES - 1:
-                break
+            if late < 0:
+                clamp(step, 0)
+            if behind >= 0:
+                stage(("b", behind))
+            if ahead < TILES:
+                stage(("e", ahead))
             if late >= 0:
-                bounce("b", late, second)
+                clamp(step, 0)
+            clamp(step, 1)
+            if late >= 0 and ahead + 1 < TILES:
+                sort_emission(ahead + 1)
+            if late >= 0:
+                bounce(("b", late), second)
+            if step + 1 < TILES:
+                bounce(("e", step + 1), direct)
+            if late >= 0:
                 finish(late)
-        turn_sent(13)
-        group(("b", 13))
-        bounce("b", 12, second)
-        if TAIL == 0:
-            quantize(("b", 13))
-            send_on_vector(15)
-            turn_sent(14)
-            group(("b", 14))
-            bounce("b", 13, second)
-            turn_sent(15)
-            group(("b", 15))
-            finish(12)
-            quantize(("b", 14))
-            bounce("b", 14, second)
-            finish(13)
-            quantize(("b", 15))
-            bounce("b", 15, second)
-            finish(14)
-            finish(15)
-        elif TAIL == 1:
-            send_on_vector(15)
-            quantize(("b", 13))
-            turn_sent(14)
-            group(("b", 14))
-            turn_sent(15)
-            group(("b", 15))
-            bounce("b", 13, second)
-            quantize(("b", 14))
-            finish(12)
-            quantize(("b", 15))
-            bounce("b", 14, second)
-            bounce("b", 15, second)
-            finish(13)
-            finish(14)
-            finish(15)
-        else:
-            quantize(("b", 13))
-            send_on_vector(15)
-            turn_sent(14)
-            group(("b", 14))
-            clamp(15, 0)
-            send_on_gpsimd(15)
-            bounce("b", 13, second)
-            finish(12)
-            finish(13, (0,))
-            quantize(("b", 14))
-            turn_sent(15)
-            group(("b", 15))
-            bounce("b", 14, second)
-            finish(13, (1,))
-            quantize(("b", 15))
-            bounce("b", 15, second)
-            finish(14)
-            finish(15)
+
+        last = TILES - 1
+        quantize(("b", last - 2))
+        for half in range(GROUPS):
+            send_on_vector(last, half)
+        turn_sent(last - 1)
+        stage(("b", last - 1))
+        bounce(("b", last - 2), second)
+        turn_sent(last)
+        stage(("b", last))
+        for i in range(last - 1, TILES):
+            quantize(("b", i))
+            bounce(("b", i), second)
+            finish(i - 1)
+        finish(last)

from contextlib import ExitStack

import concourse.mybir as mybir
from concourse.masks import make_identity

ROOMS, STATES, PATCHES = 4, 512, 1024
FLOPS = 2 * 2 * ROOMS * STATES * PATCHES * PATCHES

F32 = mybir.dt.float32
BF16 = mybir.dt.bfloat16
I32 = mybir.dt.int32
U32 = mybir.dt.uint32
U8 = mybir.dt.uint8
FP8X4 = mybir.dt.float8_e4m3fn_x4
FP4X4 = mybir.dt.float4_e2m1fn_x4
ALU = mybir.AluOpType
ACT = mybir.ActivationFunctionType

P = 128
GROUP = 512
GROUPS = PATCHES // GROUP
TILES_PER_ROOM = STATES // P
TILES = ROOMS * TILES_PER_ROOM
QUADRANTS = 4

LOAD_AHEAD = 5
TURN_DISTANCE = 2
LAG = 3
SUM_BANKS = 6
TURN_BANKS = 2


def tile_two_bounce_signed_transfer_s14_kernel(tc, emission, ff_words, ff_scales, ambient, rho, out):
    nc = tc.nc
    with ExitStack() as ctx:
        sbuf = ctx.enter_context(tc.tile_pool(name="sbuf", bufs=1))
        psum = ctx.enter_context(tc.psum_pool(name="psum", bufs=1))
        ctx.enter_context(tc.manual_schedule())

        def slot(kind, index, slots, shape, dtype):
            name = "%s%d" % (kind, index % slots)
            return sbuf.tile(shape, dtype, name=name, tag=name, align_bytes=64)

        def bank(kind, index, banks):
            name = "%s%d" % (kind, index % banks)
            return psum.tile([P, GROUP], F32, name=name, tag=name)

        identity = sbuf.tile([P, P], F32, name="identity", align_bytes=64)
        make_identity(nc, identity[:])

        first_scales = sbuf.tile([P, GROUPS * PATCHES], U8, name="first_scales", align_bytes=64)
        later_scales = sbuf.tile([P, (ROOMS - 1) * GROUPS * PATCHES], U8, name="later_scales", align_bytes=64)
        nc.vector.memset(first_scales[:].bitcast(I32), 0)
        nc.gpsimd.memset(later_scales[:].bitcast(I32), 0)

        emitted, ordered, weights, ambient_rows, rho_rows = {}, {}, {}, {}, {}
        turned, staged, codes, scales = {}, {}, {}, {}
        direct, received, clamped, sent, second = {}, {}, {}, {}, {}

        def load_emission(i):
            room, row = divmod(i, TILES_PER_ROOM)
            emitted[i] = slot("emitted", i, TILES, [P, PATCHES], BF16)
            nc.sync.dma_start(out=emitted[i][:], in_=emission[room, row * P:(row + 1) * P, :])

        def load_weights(room):
            weights[room] = slot("weights", room, ROOMS, [P, GROUPS * 2 * PATCHES], U8)
            nc.sync.dma_start(
                out=weights[room][:].bitcast(I32).rearrange("p (g n) -> p g n", g=GROUPS),
                in_=ff_words[room * GROUPS:(room + 1) * GROUPS].bitcast(I32).rearrange("g p n -> p g n"),
            )

        def load_scales(plane, first_group, groups):
            for quadrant in range(QUADRANTS):
                nc.sync.dma_start(
                    out=plane[32 * quadrant:32 * quadrant + 4, :].bitcast(I32).rearrange("q (g n) -> q g n", g=groups),
                    in_=ff_scales[first_group:first_group + groups, 4 * quadrant:4 * quadrant + 4, :]
                    .bitcast(I32).rearrange("g q n -> q g n"),
                )

        def load_row(rows, kind, source, room):
            rows[room] = slot(kind, room, 2, [P, PATCHES], BF16)
            nc.sync.dma_start(out=rows[room][:], in_=source[room].partition_broadcast(P))

        def weight_scales(room, g, half):
            if room == 0:
                plane, start = first_scales, g * PATCHES
            else:
                plane, start = later_scales, ((room - 1) * GROUPS + g) * PATCHES
            return plane[:, start + half * GROUP:start + (half + 1) * GROUP]

        def even_and_odd(groups):
            return [values.bitcast(F32)[:, odd::2] for values in groups for odd in range(2)]

        def turn(operand, quarters):
            turned[operand] = bank("turned", len(turned), TURN_BANKS)
            for n, words in enumerate(quarters):
                nc.tensor.transpose(turned[operand][:, n * P:(n + 1) * P], words, identity[:])

        def sort_emission(i):
            ordered[i] = slot("ordered", i, 2, [P, GROUP], F32)
            nc.scalar.copy(
                out=ordered[i][:].rearrange("p (g u m) -> p g u m", g=GROUPS, u=2),
                in_=emitted[i][:].bitcast(F32).rearrange("p (g m u) -> p g u m", g=GROUPS, u=2),
            )

        def turn_emission(i):
            if i in ordered:
                turn(("e", i), [ordered[i][:, n * P:(n + 1) * P] for n in range(2 * GROUPS)])
            else:
                turn(("e", i), even_and_odd([emitted[i][:, g * GROUP:(g + 1) * GROUP] for g in range(GROUPS)]))

        def turn_sent(i):
            turn(("b", i), even_and_odd([sent[i, g] for g in range(GROUPS)]))

        def staging(operand):
            return slot("staged_" + operand[0], operand[1], 2, [P, PATCHES], BF16)

        def stage(operand):
            staged[operand] = staging(operand)
            nc.scalar.copy(
                out=staged[operand][:].bitcast(F32).rearrange("p (g s u) -> p g s u", g=GROUPS, u=2),
                in_=turned[operand][:].rearrange("p (g u s) -> p g s u", g=GROUPS, u=2),
            )

        def quantize(operand):
            kind, i = operand
            codes[operand] = slot("codes_" + kind, i, 3, [P, GROUPS * P], U32)
            scales[operand] = slot("scales_" + kind, i, 3, [P, GROUPS * P], U8)
            nc.vector.quantize_mx(
                out=codes[operand][:].bitcast(FP8X4), scales=scales[operand][:], in_=staged[operand][:]
            )

        def bounce(operand, sums):
            i = operand[1]
            room = i // TILES_PER_ROOM
            for half in range(GROUPS):
                sums[i, half] = bank("sums", len(direct) + len(second), SUM_BANKS)
                for g in range(GROUPS):
                    column = g * PATCHES + half * GROUP
                    nc.tensor.matmul_mx(
                        out=sums[i, half][:],
                        lhsT=codes[operand][:, g * P:(g + 1) * P].bitcast(FP8X4),
                        lhsT_scale=scales[operand][:, g * P:(g + 1) * P],
                        rhs=weights[room][:, 2 * column:2 * (column + GROUP)].bitcast(FP4X4),
                        rhs_scale=weight_scales(room, g, half),
                        start=(g == 0),
                        stop=(g == GROUPS - 1),
                    )

        def add_ambient(i, half):
            received[i, half] = slot("received", GROUPS * i + half, 2 * GROUPS, [P, GROUP], F32)
            nc.vector.tensor_tensor(
                out=received[i, half][:],
                in0=ambient_rows[i // TILES_PER_ROOM][:, half * GROUP:(half + 1) * GROUP],
                in1=direct[i, half][:],
                op=ALU.add,
            )

        def clamp(i, half):
            clamped[i, half] = slot("clamped", GROUPS * i + half, GROUPS * (LAG + 2), [P, GROUP], F32)
            nc.scalar.activation(out=clamped[i, half][:], in_=received[i, half][:], func=ACT.Relu)

        def send(engine, i, half):
            engine.tensor_tensor(
                out=sent[i, half],
                in0=clamped[i, half][:],
                in1=rho_rows[i // TILES_PER_ROOM][:, half * GROUP:(half + 1) * GROUP],
                op=ALU.mult,
            )

        def send_on_vector(i, half):
            sent[i, half] = slot("sent", i + half, 3, [P, GROUP], BF16)[:, :]
            send(nc.vector, i, half)

        def send_on_gpsimd(i, consumed):
            sent[i, 1] = staging(consumed)[:, :GROUP]
            send(nc.gpsimd, i, 1)

        def finish(i):
            room, row = divmod(i, TILES_PER_ROOM)
            for half in range(GROUPS):
                result = slot("result", GROUPS * i + half, GROUPS * TILES, [P, GROUP], F32)
                nc.vector.tensor_tensor(out=result[:], in0=clamped[i, half][:], in1=second[i, half][:], op=ALU.add)
                nc.sync.dma_start(
                    out=out[room, row * P:(row + 1) * P, half * GROUP:(half + 1) * GROUP], in_=result[:]
                )

        load_emission(0)
        load_emission(1)
        load_scales(first_scales, 0, GROUPS)
        load_weights(0)
        load_row(ambient_rows, "ambient", ambient, 0)
        load_emission(2)
        load_row(rho_rows, "rho", rho, 0)
        for i in range(3, LOAD_AHEAD):
            load_emission(i)
        load_scales(later_scales, GROUPS, (ROOMS - 1) * GROUPS)

        for i in range(TURN_DISTANCE):
            turn_emission(i)
            stage(("e", i))
        quantize(("e", 0))
        bounce(("e", 0), direct)

        for step in range(TILES):
            room, place = divmod(step, TILES_PER_ROOM)
            ahead, behind, late = step + TURN_DISTANCE, step - TURN_DISTANCE, step - LAG
            if step + LOAD_AHEAD < TILES:
                load_emission(step + LOAD_AHEAD)
            if room + 1 < ROOMS and place == 0:
                load_weights(room + 1)
            if room + 1 < ROOMS and place == 1:
                load_row(ambient_rows, "ambient", ambient, room + 1)
            if room + 1 < ROOMS and place == 2:
                load_row(rho_rows, "rho", rho, room + 1)

            if step >= 1:
                send_on_vector(step - 1, 0)
            operands = [("b", late)] if late >= 0 else []
            if step + 1 < TILES:
                operands.append(("e", step + 1))
            for operand in operands:
                quantize(operand)
            if step >= 1:
                send_on_gpsimd(step - 1, operands[-1])

            if behind >= 0:
                turn_sent(behind)
            if ahead < TILES:
                turn_emission(ahead)
            for half in range(GROUPS):
                add_ambient(step, half)
            if late < 0:
                clamp(step, 0)
            if behind >= 0:
                stage(("b", behind))
            if ahead < TILES:
                stage(("e", ahead))
            if late >= 0:
                clamp(step, 0)
            clamp(step, 1)
            if late >= 0 and ahead + 1 < TILES:
                sort_emission(ahead + 1)
            if late >= 0:
                bounce(("b", late), second)
            if step + 1 < TILES:
                bounce(("e", step + 1), direct)
            if late >= 0:
                finish(late)

        last = TILES - 1
        quantize(("b", last - 2))
        for half in range(GROUPS):
            send_on_vector(last, half)
        turn_sent(last - 1)
        stage(("b", last - 1))
        bounce(("b", last - 2), second)
        turn_sent(last)
        stage(("b", last))
        for i in range(last - 1, TILES):
            quantize(("b", i))
            bounce(("b", i), second)
            finish(i - 1)
        finish(last)
